import numpy as np
import ml_dtypes


def mxq(x, axis, fmt="e4m3"):
    dtype, down = {"e4m3": (ml_dtypes.float8_e4m3fn, 7), "e5m2": (ml_dtypes.float8_e5m2, 14)}[fmt]
    v = np.moveaxis(np.asarray(x, np.float32).astype(ml_dtypes.bfloat16).astype(np.float64), axis, -1)
    blocks = v.reshape(v.shape[:-1] + (-1, 32))
    amax = np.abs(blocks).max(-1, keepdims=True)
    byte = np.maximum(np.where(amax > 0, np.frexp(amax)[1] - 1 + 127, 0) - down, 1)
    scale = np.exp2(byte - 127.0)
    codes = (blocks / scale).astype(np.float32).astype(dtype).astype(np.float64)
    return np.moveaxis((codes * scale).reshape(v.shape), -1, axis)


WIDE = False


def mx_kscale(k):
    if not WIDE:
        return np.ones(k)
    levels = np.array([10, -10, 5, -5, 0])
    if k % 512:
        return np.exp2(np.random.permutation(np.resize(levels, k // 32))).repeat(32)
    a = np.empty((k // 512, 16))
    for p in range(k // 512):
        a[p, :8] = np.random.permutation(np.resize(levels, 8))
        for g in range(8):
            far = levels[np.abs(levels - a[p, g]) >= 10]
            a[p, g + 8] = far[np.random.randint(len(far))]
    return np.exp2(a.ravel()).repeat(32)


def f64(x):
    return np.asarray(x).astype(np.float64)


def striped(idx):
    return np.tile(np.asarray(idx).reshape(-1, 16).T, (8, 1)).astype(np.uint16)


def unstriped(offs):
    return offs[:16].T.reshape(-1).astype(np.int64)


E2M1 = np.array([0.0, 0.5, 1.0, 1.5, 2.0, 3.0, 4.0, 6.0, -0.0, -0.5, -1.0, -1.5, -2.0, -3.0, -4.0, -6.0])


def pack_weight(w, fmt):
    k, n = w.shape
    w = f64(np.asarray(w, np.float32).astype(ml_dtypes.bfloat16)).reshape(k // 32, 32, n)
    amax = np.abs(w).max(1)
    if fmt == "e4m3":
        byte = np.frexp(amax)[1] - 1 + 127 - 7
    else:
        mant, ex = np.frexp(amax / 6.0)
        byte = np.where(mant > 0.5, ex, ex - 1) + 127
    byte = np.clip(np.where(amax > 0, byte, 1), 1, 254)
    scaled = (w * np.exp2(127.0 - byte)[:, None, :]).reshape(k, n).astype(np.float32)
    by_word = np.ascontiguousarray(scaled.reshape(k // 512, 128, 4, n).transpose(0, 1, 3, 2))
    if fmt == "e4m3":
        words = by_word.astype(ml_dtypes.float8_e4m3fn).view(np.uint8)
    else:
        c = by_word.astype(ml_dtypes.float4_e2m1fn).view(np.uint8) & 0xF
        words = (c[..., 0::2] | (c[..., 1::2] << 4)).reshape(k // 512, 128, 2 * n)
    return np.ascontiguousarray(words), np.ascontiguousarray(byte.astype(np.uint8).reshape(k // 512, 16, n))


def unpack_weight(words, scales, fmt):
    g, _, n = scales.shape
    words = np.ascontiguousarray(words).reshape(g, 128, n, -1)
    if fmt == "e4m3":
        vals = words.view(ml_dtypes.float8_e4m3fn).astype(np.float64)
    else:
        nib = np.empty((g, 128, n, 4), np.uint8)
        nib[..., 0::2] = words & 0xF
        nib[..., 1::2] = words >> 4
        vals = E2M1[nib]
    vals = vals * np.repeat(np.exp2(scales.astype(np.float64) - 127.0), 8, axis=1)[..., None]
    return vals.transpose(0, 1, 3, 2).reshape(g * 512, n)


K, L, T, J, N = 512, 512, 512, 256, 512


def setup_inputs():
    n = np.random.standard_normal
    idx = np.random.permutation(T)[:J]
    idx2 = np.random.permutation(T)[:J]
    fk = mx_kscale(K)
    fl = mx_kscale(L)
    xtp = pack_weight(n((K, T)) / fk[:, None], "e4m3")
    wp = pack_weight(n((K, N)) * 1 / np.sqrt(K) * fk[:, None], "e2m1")
    wsp = pack_weight(n((L, N)) * 1 / np.sqrt(L) * fl[:, None], "e4m3")
    return {
        "xt_words": xtp[0],
        "xt_scales": xtp[1],
        "w_words": wp[0],
        "w_scales": wp[1],
        "xs": (n((L, T)) / fl[:, None]).astype(np.float32),
        "ws_words": wsp[0],
        "ws_scales": wsp[1],
        "sh": (np.random.uniform(0.4, 1.0, (1, J))).astype(np.float32),
        "offs": striped(idx),
        "offs2": striped(idx2),
    }


def reference(xt_words, xt_scales, w_words, w_scales, xs, ws_words, ws_scales, sh, offs, offs2):
    idx = unstriped(offs)
    idx2 = unstriped(offs2)
    xtu = unpack_weight(xt_words, xt_scales, "e4m3")
    wu = unpack_weight(w_words, w_scales, "e2m1")
    wsu = unpack_weight(ws_words, ws_scales, "e4m3")
    z = wu.T @ xtu
    xsq = mxq(f64(xs), 0, "e4m3")
    s = wsu.T @ xsq
    d = f64(sh) * (z[:, idx2] - z[:, idx])
    p = np.zeros((N, T))
    p[:, idx] = d
    y = np.maximum(z + p, 0.0) + s
    return y

@@ -1,0 +1,192 @@
+from contextlib import ExitStack
+
+import concourse.mybir as mybir
+from concourse.masks import make_identity
+
+K, L, T, J, N = 512, 512, 512, 256, 512
+FLOPS = 2 * K * N * T + 2 * L * N * T
+
+F32 = mybir.dt.float32
+BF16 = mybir.dt.bfloat16
+I32 = mybir.dt.int32
+U32 = mybir.dt.uint32
+U16 = mybir.dt.uint16
+U8 = mybir.dt.uint8
+FP8X4 = mybir.dt.float8_e4m3fn_x4
+FP4X4 = mybir.dt.float4_e2m1fn_x4
+ALU = mybir.AluOpType
+ACT = mybir.ActivationFunctionType
+
+P = 128
+PACK = 4
+TILES = N // P
+BLOCKS = T // P
+
+
+def tile_list_columns_toward_partners_kernel(tc, xt_words, xt_scales, w_words, w_scales, xs, ws_words, ws_scales, sh, offs, offs2, out):
+    nc = tc.nc
+    with ExitStack() as ctx:
+        keep = ctx.enter_context(tc.tile_pool(name="keep", bufs=1))
+        psum = ctx.enter_context(tc.psum_pool(name="psum", bufs=1))
+
+        own = keep.tile([P, J // 16], U16, name="own")
+        partner = keep.tile([P, J // 16], U16, name="partner")
+        xt_codes = keep.tile([P, T], U32, name="xt_codes", align_bytes=64)
+        w_codes = keep.tile([P, 2 * N], U8, name="w_codes", align_bytes=64)
+        ws_codes = keep.tile([P, N], U32, name="ws_codes", align_bytes=64)
+        xt_plane = keep.tile([P, T], U8, name="xt_plane", align_bytes=64)
+        w_plane = keep.tile([P, N], U8, name="w_plane", align_bytes=64)
+        ws_plane = keep.tile([P, N], U8, name="ws_plane", align_bytes=64)
+        xs_codes = keep.tile([P, T], U32, name="xs_codes", align_bytes=64)
+        xs_plane = keep.tile([P, T], U8, name="xs_plane", align_bytes=64)
+        share = keep.tile([P, J], F32, name="share")
+        ident = keep.tile([P, P], F32, name="ident")
+        warm = keep.tile([P, 2], F32, name="warm")
+        pages = [keep.tile([P, T], F32, name="page%d" % m) for m in range(TILES)]
+        z = [keep.tile([P, T], F32, name="z%d" % m) for m in range(TILES)]
+        xs_raw = [keep.tile([P, PACK, T // 2], F32, name="xs_raw%d" % h) for h in range(2)]
+        xs_bf = keep.tile([P, T, PACK], BF16, name="xs_bf", tag="xs_bf", align_bytes=64)
+
+        def load_plane_quadrant(queue, plane, scales, q):
+            queue.dma_start(out=plane[32 * q : 32 * q + 4, :].bitcast(I32), in_=scales[0, 4 * q : 4 * q + 4, :].bitcast(I32))
+
+        load_plane_quadrant(nc.sync, xt_plane, xt_scales, 0)
+        load_plane_quadrant(nc.scalar, w_plane, w_scales, 0)
+        nc.sync.dma_start(out=xt_codes[:].bitcast(I32), in_=xt_words[0].rearrange("p n t -> p (n t)").bitcast(I32))
+        nc.scalar.dma_start(out=w_codes[:].bitcast(I32), in_=w_words[0].bitcast(I32))
+        for q in range(1, 4):
+            load_plane_quadrant(nc.sync, xt_plane, xt_scales, q)
+            load_plane_quadrant(nc.scalar if q < 3 else nc.sync, w_plane, w_scales, q)
+        nc.sync.dma_start(own[:], offs)
+        nc.sync.dma_start(partner[:], offs2)
+        nc.sync.dma_start(out=share[:], in_=sh[0].partition_broadcast(P))
+        xs_view = xs.rearrange("(p j) t -> p j t", j=PACK)
+        for h in range(2):
+            nc.sync.dma_start(out=xs_raw[h][:], in_=xs_view[:, :, h * (T // 2) : (h + 1) * (T // 2)])
+        nc.sync.dma_start(out=ws_codes[:].bitcast(I32), in_=ws_words[0].rearrange("p n t -> p (n t)").bitcast(I32))
+        for q in range(4):
+            load_plane_quadrant(nc.sync, ws_plane, ws_scales, q)
+
+        nc.vector.memset(warm[:, 0:1], 0.0)
+        nc.scalar.activation(out=warm[:, 1:2], in_=warm[:, 0:1], func=ACT.Relu)
+        for m in range(TILES):
+            nc.vector.memset(pages[m][:], 0.0)
+        make_identity(nc, ident[:])
+
+        for m in range(TILES):
+            z_bank = psum.tile([P, T], F32, name="z_bank%d" % m, tag="bank%d" % m)
+            nc.tensor.matmul_mx(
+                out=z_bank[:],
+                lhsT=w_codes[:, 2 * P * m : 2 * P * (m + 1)].bitcast(FP4X4),
+                lhsT_scale=w_plane[:, P * m : P * (m + 1)],
+                rhs=xt_codes[:].bitcast(FP8X4),
+                rhs_scale=xt_plane[:],
+                start=True,
+                stop=True,
+            )
+            nc.scalar.copy(out=z[m][:], in_=z_bank[:])
+
+        def add_transposed(bank, blocks, start, stop):
+            for b in range(BLOCKS):
+                nc.tensor.matmul(
+                    out=bank[:, P * b : P * (b + 1)], lhsT=blocks[:, P * b : P * (b + 1)], rhs=ident[:],
+                    is_transpose=True, start=start and b == 0, stop=stop and b == BLOCKS - 1,
+                )
+
+        picked, moved = {}, {}
+
+        def pick_own(m):
+            if m >= 2:
+                picked[m] = keep.tile([P, J], F32, name="picked%d" % m, tag="xs_bf", align_bytes=64)
+            else:
+                picked[m] = keep.tile([P, J], F32, name="picked%d" % m)
+            nc.vector.tensor_copy(out=picked[m][:], in_=z[m][:].indirect(own[:]))
+
+        def pick_partner(m):
+            moved[m] = keep.tile([P, J], F32, name="moved%d" % m)
+            nc.vector.tensor_tensor(out=moved[m][:], in0=z[m][:].indirect(partner[:]), in1=picked[m][:], op=ALU.subtract)
+
+        def place(m):
+            nc.vector.tensor_tensor(out=pages[m][:].indirect(own[:]), in0=moved[m][:], in1=share[:], op=ALU.mult)
+
+        def quantize_xs():
+            for h in range(2):
+                dst = xs_bf[:, h * (T // 2) : (h + 1) * (T // 2), :]
+                nc.scalar.copy(out=dst.rearrange("p (c i) j -> p c j i", i=4), in_=xs_raw[h][:].rearrange("p j (c i) -> p c j i", i=4))
+            nc.vector.quantize_mx(out=xs_codes[:].bitcast(FP8X4), scales=xs_plane[:], in_=xs_bf[:].rearrange("p t j -> p (t j)"))
+
+        s_t, u_bank = {}, {}
+
+        def second_product_transposed(m):
+            bank = psum.tile([P, T], F32, name="st_bank%d" % m, tag="bank%d" % m)
+            for b in range(BLOCKS):
+                nc.tensor.matmul_mx(
+                    out=bank[:, P * b : P * (b + 1)],
+                    lhsT=xs_codes[:, P * b : P * (b + 1)].bitcast(FP8X4),
+                    lhsT_scale=xs_plane[:, P * b : P * (b + 1)],
+                    rhs=ws_codes[:, P * m : P * (m + 1)].bitcast(FP8X4),
+                    rhs_scale=ws_plane[:, P * m : P * (m + 1)],
+                    start=True,
+                    stop=True,
+                )
+            s_t[m] = keep.tile([P, T], F32, name="s_t%d" % m)
+            nc.scalar.copy(out=s_t[m][:], in_=bank[:])
+
+        relu_t = {}
+
+        def mix_transposed(m):
+            bank = psum.tile([P, T], F32, name="u_bank%d" % m, tag="bank%d" % (4 + m % 2))
+            add_transposed(bank, z[m], True, False)
+            add_transposed(bank, pages[m], False, True)
+            relu_t[m] = keep.tile([P, T], F32, name="relu_t%d" % m)
+            nc.scalar.activation(out=relu_t[m][:], in_=bank[:], func=ACT.Relu)
+
+        def finish_transposed(m):
+            bank = psum.tile([P, T], F32, name="y_bank%d" % m, tag="bank%d" % (6 + m % 2))
+            add_transposed(bank, relu_t[m], True, False)
+            add_transposed(bank, s_t[m], False, True)
+            y = keep.tile([P, T], F32, name="y%d" % m)
+            nc.scalar.copy(out=y[:], in_=bank[:])
+            nc.scalar.dma_start(out=out[P * m : P * (m + 1), :], in_=y[:])
+
+        last = TILES - 1
+        pick_own(0)
+        pick_partner(0)
+        pick_own(1)
+        place(0)
+        pick_partner(1)
+        quantize_xs()
+        mix_transposed(0)
+        pick_own(2)
+        place(1)
+        for m in range(last):
+            second_product_transposed(m)
+        s_bank = psum.tile([P, T], F32, name="s_bank", tag="bank%d" % last)
+        nc.tensor.matmul_mx(
+            out=s_bank[:],
+            lhsT=ws_codes[:, P * last :].bitcast(FP8X4),
+            lhsT_scale=ws_plane[:, P * last :],
+            rhs=xs_codes[:].bitcast(FP8X4),
+            rhs_scale=xs_plane[:],
+            start=True,
+            stop=True,
+        )
+        finish_transposed(0)
+        pick_partner(2)
+        mix_transposed(1)
+        finish_transposed(1)
+        pick_own(3)
+        place(2)
+        pick_partner(3)
+        mix_transposed(2)
+        finish_transposed(2)
+        place(3)
+
+        halves = [slice(h * (T // 2), (h + 1) * (T // 2)) for h in range(2)]
+        mixed = [keep.tile([P, T // 2], F32, name="mixed%d" % h) for h in range(2)]
+        y_last = [keep.tile([P, T // 2], F32, name="y_last%d" % h) for h in range(2)]
+        for h in range(2):
+            nc.vector.tensor_tensor(out=mixed[h][:], in0=z[last][:, halves[h]], in1=pages[last][:, halves[h]], op=ALU.add)
+        for h, queue in enumerate((nc.sync, nc.sync)):
+            nc.vector.scalar_tensor_tensor(out=y_last[h][:], in0=mixed[h][:], scalar=0.0, in1=s_bank[:, halves[h]], op0=ALU.max, op1=ALU.add)
+            queue.dma_start(out=out[P * last :, halves[h]], in_=y_last[h][:])

@@ -27,6 +27,7 @@ def tile_list_columns_toward_partners_kernel(tc, xt_words, xt_scales, w_words, w
     nc = tc.nc
     with ExitStack() as ctx:
         keep = ctx.enter_context(tc.tile_pool(name="keep", bufs=1))
+        reused = ctx.enter_context(tc.tile_pool(name="reused", bufs=1))
         psum = ctx.enter_context(tc.psum_pool(name="psum", bufs=1))
 
         own = keep.tile([P, J // 16], U16, name="own")
@@ -40,12 +41,14 @@ def tile_list_columns_toward_partners_kernel(tc, xt_words, xt_scales, w_words, w
         xs_codes = keep.tile([P, T], U32, name="xs_codes", align_bytes=64)
         xs_plane = keep.tile([P, T], U8, name="xs_plane", align_bytes=64)
         share = keep.tile([P, J], F32, name="share")
+        share_cols = keep.tile([P, J // P], F32, name="share_cols")
         ident = keep.tile([P, P], F32, name="ident")
         warm = keep.tile([P, 2], F32, name="warm")
         pages = [keep.tile([P, T], F32, name="page%d" % m) for m in range(TILES)]
-        z = [keep.tile([P, T], F32, name="z%d" % m) for m in range(TILES)]
-        xs_raw = [keep.tile([P, PACK, T // 2], F32, name="xs_raw%d" % h) for h in range(2)]
-        xs_bf = keep.tile([P, T, PACK], BF16, name="xs_bf", tag="xs_bf", align_bytes=64)
+        z = [keep.tile([P, T], F32, name="z%d" % m) for m in range(2)]
+        z = z + [reused.tile([P, T], F32, name="z%d" % m, offset=8192 + 2048 * (m - 2)) for m in range(2, TILES)]
+        xs_raw = [reused.tile([P, PACK, T // 2], F32, name="xs_raw%d" % h, offset=4096 * (h + 1)) for h in range(2)]
+        xs_bf = reused.tile([P, T, PACK], BF16, name="xs_bf", align_bytes=64, offset=0)
 
         def load_plane_quadrant(queue, plane, scales, q):
             queue.dma_start(out=plane[32 * q : 32 * q + 4, :].bitcast(I32), in_=scales[0, 4 * q : 4 * q + 4, :].bitcast(I32))
@@ -59,7 +62,7 @@ def tile_list_columns_toward_partners_kernel(tc, xt_words, xt_scales, w_words, w
             load_plane_quadrant(nc.scalar if q < 3 else nc.sync, w_plane, w_scales, q)
         nc.sync.dma_start(own[:], offs)
         nc.sync.dma_start(partner[:], offs2)
-        nc.sync.dma_start(out=share[:], in_=sh[0].partition_broadcast(P))
+        nc.sync.dma_start(out=share_cols[:], in_=sh[0].rearrange("(p c) -> p c", c=J // P))
         xs_view = xs.rearrange("(p j) t -> p j t", j=PACK)
         for h in range(2):
             nc.sync.dma_start(out=xs_raw[h][:], in_=xs_view[:, :, h * (T // 2) : (h + 1) * (T // 2)])
@@ -73,41 +76,52 @@ def tile_list_columns_toward_partners_kernel(tc, xt_words, xt_scales, w_words, w
             nc.vector.memset(pages[m][:], 0.0)
         make_identity(nc, ident[:])
 
-        for m in range(TILES):
-            z_bank = psum.tile([P, T], F32, name="z_bank%d" % m, tag="bank%d" % m)
+        def first_product(m, cols, tag, copy):
+            bank = psum.tile([P, cols.stop - cols.start], F32, name="z_bank%d_%d" % (m, cols.start), tag=tag)
             nc.tensor.matmul_mx(
-                out=z_bank[:],
+                out=bank[:],
                 lhsT=w_codes[:, 2 * P * m : 2 * P * (m + 1)].bitcast(FP4X4),
                 lhsT_scale=w_plane[:, P * m : P * (m + 1)],
-                rhs=xt_codes[:].bitcast(FP8X4),
-                rhs_scale=xt_plane[:],
+                rhs=xt_codes[:, cols].bitcast(FP8X4),
+                rhs_scale=xt_plane[:, cols],
                 start=True,
                 stop=True,
             )
-            nc.scalar.copy(out=z[m][:], in_=z_bank[:])
+            return lambda: copy(out=z[m][:, cols], in_=bank[:])
 
-        def add_transposed(bank, blocks, start, stop):
-            for b in range(BLOCKS):
+        halves = [slice(h * (T // 2), (h + 1) * (T // 2)) for h in range(2)]
+        first_product(0, halves[0], "bank0", nc.vector.tensor_copy)()
+        first_product(0, halves[1], "bank4", nc.scalar.copy)()
+        copy_z = {m: first_product(m, slice(0, T), "bank%d" % m, nc.scalar.copy) for m in range(1, TILES)}
+        copy_z[1]()
+
+        share_bank = psum.tile([P, J // P, P], F32, name="share_bank", tag="bank0")
+        for c in range(J // P):
+            nc.tensor.transpose(share_bank[:, c, :], share_cols[:, c : c + 1].to_broadcast([P, P]), ident[:])
+        nc.scalar.copy(out=share[:].rearrange("p (n c) -> p n c", c=J // P), in_=share_bank[:].rearrange("p c n -> p n c"))
+
+        def add_transposed(bank, source, blocks, start, stop):
+            for i, b in enumerate(blocks):
                 nc.tensor.matmul(
-                    out=bank[:, P * b : P * (b + 1)], lhsT=blocks[:, P * b : P * (b + 1)], rhs=ident[:],
-                    is_transpose=True, start=start and b == 0, stop=stop and b == BLOCKS - 1,
+                    out=bank[:, P * i : P * (i + 1)], lhsT=source[:, P * b : P * (b + 1)], rhs=ident[:],
+                    is_transpose=True, start=start and i == 0, stop=stop and i == len(blocks) - 1,
                 )
 
-        picked, moved = {}, {}
+        picked, gaps = {}, {}
 
         def pick_own(m):
-            if m >= 2:
-                picked[m] = keep.tile([P, J], F32, name="picked%d" % m, tag="xs_bf", align_bytes=64)
-            else:
-                picked[m] = keep.tile([P, J], F32, name="picked%d" % m)
+            picked[m] = keep.tile([P, J], F32, name="picked%d" % m)
             nc.vector.tensor_copy(out=picked[m][:], in_=z[m][:].indirect(own[:]))
 
         def pick_partner(m):
-            moved[m] = keep.tile([P, J], F32, name="moved%d" % m)
-            nc.vector.tensor_tensor(out=moved[m][:], in0=z[m][:].indirect(partner[:]), in1=picked[m][:], op=ALU.subtract)
+            if m == 1:
+                gaps[m] = reused.tile([P, J], F32, name="gap%d" % m, offset=0)
+            else:
+                gaps[m] = keep.tile([P, J], F32, name="gap%d" % m)
+            nc.vector.tensor_tensor(out=gaps[m][:], in0=z[m][:].indirect(partner[:]), in1=picked[m][:], op=ALU.subtract)
 
         def place(m):
-            nc.vector.tensor_tensor(out=pages[m][:].indirect(own[:]), in0=moved[m][:], in1=share[:], op=ALU.mult)
+            nc.vector.tensor_tensor(out=pages[m][:].indirect(own[:]), in0=gaps[m][:], in1=share[:], op=ALU.mult)
 
         def quantize_xs():
             for h in range(2):
@@ -134,33 +148,46 @@ def tile_list_columns_toward_partners_kernel(tc, xt_words, xt_scales, w_words, w
 
         relu_t = {}
 
-        def mix_transposed(m):
-            bank = psum.tile([P, T], F32, name="u_bank%d" % m, tag="bank%d" % (4 + m % 2))
-            add_transposed(bank, z[m], True, False)
-            add_transposed(bank, pages[m], False, True)
-            relu_t[m] = keep.tile([P, T], F32, name="relu_t%d" % m)
-            nc.scalar.activation(out=relu_t[m][:], in_=bank[:], func=ACT.Relu)
+        def mix_transposed(m, blocks, tag):
+            width = P * len(blocks)
+            bank = psum.tile([P, width], F32, name="u_bank%d_%d" % (m, blocks[0]), tag=tag)
+            add_transposed(bank, z[m], blocks, True, False)
+            add_transposed(bank, pages[m], blocks, False, True)
+            if m == 0:
+                relu = reused.tile([P, width], F32, name="relu_t0", offset=2048)
+            else:
+                relu = keep.tile([P, width], F32, name="relu_t%d_%d" % (m, blocks[0]))
+            nc.scalar.activation(out=relu[:], in_=bank[:], func=ACT.Relu)
+            relu_t[m, blocks[0]] = relu
 
-        def finish_transposed(m):
-            bank = psum.tile([P, T], F32, name="y_bank%d" % m, tag="bank%d" % (6 + m % 2))
-            add_transposed(bank, relu_t[m], True, False)
-            add_transposed(bank, s_t[m], False, True)
-            y = keep.tile([P, T], F32, name="y%d" % m)
+        def finish_transposed(m, blocks, tag):
+            width = P * len(blocks)
+            bank = psum.tile([P, width], F32, name="y_bank%d_%d" % (m, blocks[0]), tag=tag)
+            add_transposed(bank, s_t[m], blocks, True, False)
+            add_transposed(bank, relu_t[m, blocks[0]], range(len(blocks)), False, True)
+            y = keep.tile([P, width], F32, name="y%d_%d" % (m, blocks[0]))
             nc.scalar.copy(out=y[:], in_=bank[:])
-            nc.scalar.dma_start(out=out[P * m : P * (m + 1), :], in_=y[:])
+            nc.scalar.dma_start(out=out[P * m : P * (m + 1), P * blocks[0] : P * blocks[0] + width], in_=y[:])
 
         last = TILES - 1
+        whole = range(BLOCKS)
         pick_own(0)
         pick_partner(0)
         pick_own(1)
         place(0)
-        pick_partner(1)
         quantize_xs()
-        mix_transposed(0)
+        pick_partner(1)
+        copy_z[2]()
+        copy_z[3]()
+        mix_transposed(0, whole, "bank4")
         pick_own(2)
         place(1)
+        pick_partner(2)
         for m in range(last):
             second_product_transposed(m)
+        finish_transposed(0, whole, "bank6")
+        mix_transposed(1, whole, "bank5")
+        finish_transposed(1, whole, "bank7")
         s_bank = psum.tile([P, T], F32, name="s_bank", tag="bank%d" % last)
         nc.tensor.matmul_mx(
             out=s_bank[:],
@@ -171,18 +198,15 @@ def tile_list_columns_toward_partners_kernel(tc, xt_words, xt_scales, w_words, w
             start=True,
             stop=True,
         )
-        finish_transposed(0)
-        pick_partner(2)
-        mix_transposed(1)
-        finish_transposed(1)
         pick_own(3)
         place(2)
         pick_partner(3)
-        mix_transposed(2)
-        finish_transposed(2)
+        mix_transposed(2, range(0, 2), "bank5")
+        mix_transposed(2, range(2, 4), "bank7")
+        finish_transposed(2, range(0, 2), "bank4")
+        finish_transposed(2, range(2, 4), "bank0")
         place(3)
 
-        halves = [slice(h * (T // 2), (h + 1) * (T // 2)) for h in range(2)]
         mixed = [keep.tile([P, T // 2], F32, name="mixed%d" % h) for h in range(2)]
         y_last = [keep.tile([P, T // 2], F32, name="y_last%d" % h) for h in range(2)]
         for h in range(2):

@@ -55,14 +55,17 @@ def tile_list_columns_toward_partners_kernel(tc, xt_words, xt_scales, w_words, w
 
         load_plane_quadrant(nc.sync, xt_plane, xt_scales, 0)
         load_plane_quadrant(nc.scalar, w_plane, w_scales, 0)
+        nc.sync.dma_start(own[:], offs)
+        load_plane_quadrant(nc.scalar, w_plane, w_scales, 1)
         nc.sync.dma_start(out=xt_codes[:].bitcast(I32), in_=xt_words[0].rearrange("p n t -> p (n t)").bitcast(I32))
         nc.scalar.dma_start(out=w_codes[:].bitcast(I32), in_=w_words[0].bitcast(I32))
-        for q in range(1, 4):
-            load_plane_quadrant(nc.sync, xt_plane, xt_scales, q)
-            load_plane_quadrant(nc.scalar if q < 3 else nc.sync, w_plane, w_scales, q)
-        nc.sync.dma_start(own[:], offs)
+        load_plane_quadrant(nc.sync, xt_plane, xt_scales, 1)
+        load_plane_quadrant(nc.scalar, w_plane, w_scales, 2)
+        load_plane_quadrant(nc.sync, xt_plane, xt_scales, 2)
+        load_plane_quadrant(nc.sync, xt_plane, xt_scales, 3)
+        load_plane_quadrant(nc.sync, w_plane, w_scales, 3)
         nc.sync.dma_start(partner[:], offs2)
-        nc.sync.dma_start(out=share_cols[:], in_=sh[0].rearrange("(p c) -> p c", c=J // P))
+        nc.gpsimd.dma_start(out=share_cols[:], in_=sh[0].rearrange("(p c) -> p c", c=J // P))
         xs_view = xs.rearrange("(p j) t -> p j t", j=PACK)
         for h in range(2):
             nc.sync.dma_start(out=xs_raw[h][:], in_=xs_view[:, :, h * (T // 2) : (h + 1) * (T // 2)])
@@ -90,8 +93,9 @@ def tile_list_columns_toward_partners_kernel(tc, xt_words, xt_scales, w_words, w
             return lambda: copy(out=z[m][:, cols], in_=bank[:])
 
         halves = [slice(h * (T // 2), (h + 1) * (T // 2)) for h in range(2)]
-        first_product(0, halves[0], "bank0", nc.vector.tensor_copy)()
-        first_product(0, halves[1], "bank4", nc.scalar.copy)()
+        first_product(0, slice(0, 256), "bank0", nc.scalar.copy)()
+        first_product(0, slice(256, 384), "bank4", nc.vector.tensor_copy)()
+        first_product(0, slice(384, 512), "bank5", nc.vector.tensor_copy)()
         copy_z = {m: first_product(m, slice(0, T), "bank%d" % m, nc.scalar.copy) for m in range(1, TILES)}
         copy_z[1]()
 
@@ -207,10 +211,11 @@ def tile_list_columns_toward_partners_kernel(tc, xt_words, xt_scales, w_words, w
         finish_transposed(2, range(2, 4), "bank0")
         place(3)
 
-        mixed = [keep.tile([P, T // 2], F32, name="mixed%d" % h) for h in range(2)]
-        y_last = [keep.tile([P, T // 2], F32, name="y_last%d" % h) for h in range(2)]
+        parts = [slice(0, 320), slice(320, T)]
+        mixed = [keep.tile([P, c.stop - c.start], F32, name="mixed%d" % c.start) for c in parts]
+        y_last = [keep.tile([P, c.stop - c.start], F32, name="y_last%d" % c.start) for c in parts]
         for h in range(2):
-            nc.vector.tensor_tensor(out=mixed[h][:], in0=z[last][:, halves[h]], in1=pages[last][:, halves[h]], op=ALU.add)
-        for h, queue in enumerate((nc.sync, nc.sync)):
-            nc.vector.scalar_tensor_tensor(out=y_last[h][:], in0=mixed[h][:], scalar=0.0, in1=s_bank[:, halves[h]], op0=ALU.max, op1=ALU.add)
-            queue.dma_start(out=out[P * last :, halves[h]], in_=y_last[h][:])
+            nc.vector.tensor_tensor(out=mixed[h][:], in0=z[last][:, parts[h]], in1=pages[last][:, parts[h]], op=ALU.add)
+        for h in range(2):
+            nc.vector.scalar_tensor_tensor(out=y_last[h][:], in0=mixed[h][:], scalar=0.0, in1=s_bank[:, parts[h]], op0=ALU.max, op1=ALU.add)
+            nc.sync.dma_start(out=out[P * last :, parts[h]], in_=y_last[h][:])

@@ -61,11 +61,11 @@ def tile_list_columns_toward_partners_kernel(tc, xt_words, xt_scales, w_words, w
         nc.scalar.dma_start(out=w_codes[:].bitcast(I32), in_=w_words[0].bitcast(I32))
         load_plane_quadrant(nc.sync, xt_plane, xt_scales, 1)
         load_plane_quadrant(nc.scalar, w_plane, w_scales, 2)
+        nc.scalar.dma_start(out=share_cols[:], in_=sh[0].rearrange("(p c) -> p c", c=J // P))
         load_plane_quadrant(nc.sync, xt_plane, xt_scales, 2)
         load_plane_quadrant(nc.sync, xt_plane, xt_scales, 3)
         load_plane_quadrant(nc.sync, w_plane, w_scales, 3)
         nc.sync.dma_start(partner[:], offs2)
-        nc.gpsimd.dma_start(out=share_cols[:], in_=sh[0].rearrange("(p c) -> p c", c=J // P))
         xs_view = xs.rearrange("(p j) t -> p j t", j=PACK)
         for h in range(2):
             nc.sync.dma_start(out=xs_raw[h][:], in_=xs_view[:, :, h * (T // 2) : (h + 1) * (T // 2)])
@@ -128,9 +128,11 @@ def tile_list_columns_toward_partners_kernel(tc, xt_words, xt_scales, w_words, w
             nc.vector.tensor_tensor(out=pages[m][:].indirect(own[:]), in0=gaps[m][:], in1=share[:], op=ALU.mult)
 
         def quantize_xs():
-            for h in range(2):
-                dst = xs_bf[:, h * (T // 2) : (h + 1) * (T // 2), :]
-                nc.scalar.copy(out=dst.rearrange("p (c i) j -> p c j i", i=4), in_=xs_raw[h][:].rearrange("p j (c i) -> p c j i", i=4))
+            quarter = T // 4
+            for c in range(4):
+                dst = xs_bf[:, c * quarter : (c + 1) * quarter, :]
+                src = xs_raw[c // 2][:, :, (c % 2) * quarter : (c % 2 + 1) * quarter]
+                nc.scalar.copy(out=dst.rearrange("p (c i) j -> p c j i", i=4), in_=src.rearrange("p j (c i) -> p c j i", i=4))
             nc.vector.quantize_mx(out=xs_codes[:].bitcast(FP8X4), scales=xs_plane[:], in_=xs_bf[:].rearrange("p t j -> p (t j)"))
 
         s_t, u_bank = {}, {}

@@ -19,8 +19,22 @@ ACT = mybir.ActivationFunctionType
 
 P = 128
 PACK = 4
+QUADRANTS = 4
+GROUP = 16
 TILES = N // P
 BLOCKS = T // P
+LAST = TILES - 1
+SHARES = J // P
+RUN = 4
+ROUND_PIECES = 4
+LAST_SPLIT = 320
+
+ROW_BYTES = 4 * T
+XS_BF_AT = 0
+XS_RAW_AT = (2 * ROW_BYTES, 4 * ROW_BYTES)
+GAP1_AT = XS_BF_AT
+RELU0_AT = XS_BF_AT + ROW_BYTES
+Z_LATE_AT = XS_RAW_AT[1]
 
 
 def tile_list_columns_toward_partners_kernel(tc, xt_words, xt_scales, w_words, w_scales, xs, ws_words, ws_scales, sh, offs, offs2, out):
@@ -30,8 +44,8 @@ def tile_list_columns_toward_partners_kernel(tc, xt_words, xt_scales, w_words, w
         reused = ctx.enter_context(tc.tile_pool(name="reused", bufs=1))
         psum = ctx.enter_context(tc.psum_pool(name="psum", bufs=1))
 
-        own = keep.tile([P, J // 16], U16, name="own")
-        partner = keep.tile([P, J // 16], U16, name="partner")
+        own = keep.tile([P, J // GROUP], U16, name="own")
+        partner = keep.tile([P, J // GROUP], U16, name="partner")
         xt_codes = keep.tile([P, T], U32, name="xt_codes", align_bytes=64)
         w_codes = keep.tile([P, 2 * N], U8, name="w_codes", align_bytes=64)
         ws_codes = keep.tile([P, N], U32, name="ws_codes", align_bytes=64)
@@ -41,14 +55,13 @@ def tile_list_columns_toward_partners_kernel(tc, xt_words, xt_scales, w_words, w
         xs_codes = keep.tile([P, T], U32, name="xs_codes", align_bytes=64)
         xs_plane = keep.tile([P, T], U8, name="xs_plane", align_bytes=64)
         share = keep.tile([P, J], F32, name="share")
-        share_cols = keep.tile([P, J // P], F32, name="share_cols")
+        share_cols = keep.tile([P, SHARES], F32, name="share_cols")
         ident = keep.tile([P, P], F32, name="ident")
-        warm = keep.tile([P, 2], F32, name="warm")
         pages = [keep.tile([P, T], F32, name="page%d" % m) for m in range(TILES)]
         z = [keep.tile([P, T], F32, name="z%d" % m) for m in range(2)]
-        z = z + [reused.tile([P, T], F32, name="z%d" % m, offset=8192 + 2048 * (m - 2)) for m in range(2, TILES)]
-        xs_raw = [reused.tile([P, PACK, T // 2], F32, name="xs_raw%d" % h, offset=4096 * (h + 1)) for h in range(2)]
-        xs_bf = reused.tile([P, T, PACK], BF16, name="xs_bf", align_bytes=64, offset=0)
+        z = z + [reused.tile([P, T], F32, name="z%d" % m, offset=Z_LATE_AT + ROW_BYTES * (m - 2)) for m in range(2, TILES)]
+        xs_raw = [reused.tile([P, PACK, T // 2], F32, name="xs_raw%d" % h, offset=XS_RAW_AT[h]) for h in range(2)]
+        xs_bf = reused.tile([P, T, PACK], BF16, name="xs_bf", align_bytes=64, offset=XS_BF_AT)
 
         def load_plane_quadrant(queue, plane, scales, q):
             queue.dma_start(out=plane[32 * q : 32 * q + 4, :].bitcast(I32), in_=scales[0, 4 * q : 4 * q + 4, :].bitcast(I32))
@@ -61,7 +74,7 @@ def tile_list_columns_toward_partners_kernel(tc, xt_words, xt_scales, w_words, w
         nc.scalar.dma_start(out=w_codes[:].bitcast(I32), in_=w_words[0].bitcast(I32))
         load_plane_quadrant(nc.sync, xt_plane, xt_scales, 1)
         load_plane_quadrant(nc.scalar, w_plane, w_scales, 2)
-        nc.scalar.dma_start(out=share_cols[:], in_=sh[0].rearrange("(p c) -> p c", c=J // P))
+        nc.scalar.dma_start(out=share_cols[:], in_=sh[0].rearrange("(p c) -> p c", c=SHARES))
         load_plane_quadrant(nc.sync, xt_plane, xt_scales, 2)
         load_plane_quadrant(nc.sync, xt_plane, xt_scales, 3)
         load_plane_quadrant(nc.sync, w_plane, w_scales, 3)
@@ -70,16 +83,14 @@ def tile_list_columns_toward_partners_kernel(tc, xt_words, xt_scales, w_words, w
         for h in range(2):
             nc.sync.dma_start(out=xs_raw[h][:], in_=xs_view[:, :, h * (T // 2) : (h + 1) * (T // 2)])
         nc.sync.dma_start(out=ws_codes[:].bitcast(I32), in_=ws_words[0].rearrange("p n t -> p (n t)").bitcast(I32))
-        for q in range(4):
+        for q in range(QUADRANTS):
             load_plane_quadrant(nc.sync, ws_plane, ws_scales, q)
 
-        nc.vector.memset(warm[:, 0:1], 0.0)
-        nc.scalar.activation(out=warm[:, 1:2], in_=warm[:, 0:1], func=ACT.Relu)
         for m in range(TILES):
             nc.vector.memset(pages[m][:], 0.0)
         make_identity(nc, ident[:])
 
-        def first_product(m, cols, tag, copy):
+        def first_product(m, cols, tag):
             bank = psum.tile([P, cols.stop - cols.start], F32, name="z_bank%d_%d" % (m, cols.start), tag=tag)
             nc.tensor.matmul_mx(
                 out=bank[:],
@@ -90,19 +101,23 @@ def tile_list_columns_toward_partners_kernel(tc, xt_words, xt_scales, w_words, w
                 start=True,
                 stop=True,
             )
-            return lambda: copy(out=z[m][:, cols], in_=bank[:])
+            return bank
 
-        halves = [slice(h * (T // 2), (h + 1) * (T // 2)) for h in range(2)]
-        first_product(0, slice(0, 256), "bank0", nc.scalar.copy)()
-        first_product(0, slice(256, 384), "bank4", nc.vector.tensor_copy)()
-        first_product(0, slice(384, 512), "bank5", nc.vector.tensor_copy)()
-        copy_z = {m: first_product(m, slice(0, T), "bank%d" % m, nc.scalar.copy) for m in range(1, TILES)}
-        copy_z[1]()
+        half, quarters = slice(0, T // 2), (slice(T // 2, 3 * T // 4), slice(3 * T // 4, T))
+        nc.scalar.activation(out=z[0][:, half], in_=first_product(0, half, "bank0")[:], func=ACT.Copy)
+        for cols, tag in zip(quarters, ("bank4", "bank5")):
+            nc.vector.tensor_copy(out=z[0][:, cols], in_=first_product(0, cols, tag)[:])
+        z_banks = {m: first_product(m, slice(0, T), "bank%d" % m) for m in range(1, TILES)}
 
-        share_bank = psum.tile([P, J // P, P], F32, name="share_bank", tag="bank0")
-        for c in range(J // P):
+        def copy_z(m):
+            nc.scalar.copy(out=z[m][:], in_=z_banks[m][:])
+
+        copy_z(1)
+
+        share_bank = psum.tile([P, SHARES, P], F32, name="share_bank", tag="bank0")
+        for c in range(SHARES):
             nc.tensor.transpose(share_bank[:, c, :], share_cols[:, c : c + 1].to_broadcast([P, P]), ident[:])
-        nc.scalar.copy(out=share[:].rearrange("p (n c) -> p n c", c=J // P), in_=share_bank[:].rearrange("p c n -> p n c"))
+        nc.scalar.copy(out=share[:].rearrange("p (n c) -> p n c", c=SHARES), in_=share_bank[:].rearrange("p c n -> p n c"))
 
         def add_transposed(bank, source, blocks, start, stop):
             for i, b in enumerate(blocks):
@@ -111,7 +126,7 @@ def tile_list_columns_toward_partners_kernel(tc, xt_words, xt_scales, w_words, w
                     is_transpose=True, start=start and i == 0, stop=stop and i == len(blocks) - 1,
                 )
 
-        picked, gaps = {}, {}
+        picked, gaps, s_t, relu_t = {}, {}, {}, {}
 
         def pick_own(m):
             picked[m] = keep.tile([P, J], F32, name="picked%d" % m)
@@ -119,7 +134,7 @@ def tile_list_columns_toward_partners_kernel(tc, xt_words, xt_scales, w_words, w
 
         def pick_partner(m):
             if m == 1:
-                gaps[m] = reused.tile([P, J], F32, name="gap%d" % m, offset=0)
+                gaps[m] = reused.tile([P, J], F32, name="gap%d" % m, offset=GAP1_AT)
             else:
                 gaps[m] = keep.tile([P, J], F32, name="gap%d" % m)
             nc.vector.tensor_tensor(out=gaps[m][:], in0=z[m][:].indirect(partner[:]), in1=picked[m][:], op=ALU.subtract)
@@ -128,14 +143,13 @@ def tile_list_columns_toward_partners_kernel(tc, xt_words, xt_scales, w_words, w
             nc.vector.tensor_tensor(out=pages[m][:].indirect(own[:]), in0=gaps[m][:], in1=share[:], op=ALU.mult)
 
         def quantize_xs():
-            quarter = T // 4
-            for c in range(4):
-                dst = xs_bf[:, c * quarter : (c + 1) * quarter, :]
-                src = xs_raw[c // 2][:, :, (c % 2) * quarter : (c % 2 + 1) * quarter]
-                nc.scalar.copy(out=dst.rearrange("p (c i) j -> p c j i", i=4), in_=src.rearrange("p j (c i) -> p c j i", i=4))
+            width = T // ROUND_PIECES
+            per_half = ROUND_PIECES // 2
+            for c in range(ROUND_PIECES):
+                dst = xs_bf[:, c * width : (c + 1) * width, :]
+                src = xs_raw[c // per_half][:, :, (c % per_half) * width : (c % per_half + 1) * width]
+                nc.scalar.copy(out=dst.rearrange("p (c i) j -> p c j i", i=RUN), in_=src.rearrange("p j (c i) -> p c j i", i=RUN))
             nc.vector.quantize_mx(out=xs_codes[:].bitcast(FP8X4), scales=xs_plane[:], in_=xs_bf[:].rearrange("p t j -> p (t j)"))
-
-        s_t, u_bank = {}, {}
 
         def second_product_transposed(m):
             bank = psum.tile([P, T], F32, name="st_bank%d" % m, tag="bank%d" % m)
@@ -152,15 +166,13 @@ def tile_list_columns_toward_partners_kernel(tc, xt_words, xt_scales, w_words, w
             s_t[m] = keep.tile([P, T], F32, name="s_t%d" % m)
             nc.scalar.copy(out=s_t[m][:], in_=bank[:])
 
-        relu_t = {}
-
         def mix_transposed(m, blocks, tag):
             width = P * len(blocks)
             bank = psum.tile([P, width], F32, name="u_bank%d_%d" % (m, blocks[0]), tag=tag)
             add_transposed(bank, z[m], blocks, True, False)
             add_transposed(bank, pages[m], blocks, False, True)
             if m == 0:
-                relu = reused.tile([P, width], F32, name="relu_t0", offset=2048)
+                relu = reused.tile([P, width], F32, name="relu_t0", offset=RELU0_AT)
             else:
                 relu = keep.tile([P, width], F32, name="relu_t%d_%d" % (m, blocks[0]))
             nc.scalar.activation(out=relu[:], in_=bank[:], func=ACT.Relu)
@@ -175,7 +187,6 @@ def tile_list_columns_toward_partners_kernel(tc, xt_words, xt_scales, w_words, w
             nc.scalar.copy(out=y[:], in_=bank[:])
             nc.scalar.dma_start(out=out[P * m : P * (m + 1), P * blocks[0] : P * blocks[0] + width], in_=y[:])
 
-        last = TILES - 1
         whole = range(BLOCKS)
         pick_own(0)
         pick_partner(0)
@@ -183,22 +194,22 @@ def tile_list_columns_toward_partners_kernel(tc, xt_words, xt_scales, w_words, w
         place(0)
         quantize_xs()
         pick_partner(1)
-        copy_z[2]()
-        copy_z[3]()
+        copy_z(2)
+        copy_z(3)
         mix_transposed(0, whole, "bank4")
         pick_own(2)
         place(1)
         pick_partner(2)
-        for m in range(last):
+        for m in range(LAST):
             second_product_transposed(m)
         finish_transposed(0, whole, "bank6")
         mix_transposed(1, whole, "bank5")
         finish_transposed(1, whole, "bank7")
-        s_bank = psum.tile([P, T], F32, name="s_bank", tag="bank%d" % last)
+        s_bank = psum.tile([P, T], F32, name="s_bank", tag="bank%d" % LAST)
         nc.tensor.matmul_mx(
             out=s_bank[:],
-            lhsT=ws_codes[:, P * last :].bitcast(FP8X4),
-            lhsT_scale=ws_plane[:, P * last :],
+            lhsT=ws_codes[:, P * LAST :].bitcast(FP8X4),
+            lhsT_scale=ws_plane[:, P * LAST :],
             rhs=xs_codes[:].bitcast(FP8X4),
             rhs_scale=xs_plane[:],
             start=True,
@@ -207,17 +218,18 @@ def tile_list_columns_toward_partners_kernel(tc, xt_words, xt_scales, w_words, w
         pick_own(3)
         place(2)
         pick_partner(3)
-        mix_transposed(2, range(0, 2), "bank5")
-        mix_transposed(2, range(2, 4), "bank7")
-        finish_transposed(2, range(0, 2), "bank4")
-        finish_transposed(2, range(2, 4), "bank0")
+        front, back = range(0, BLOCKS // 2), range(BLOCKS // 2, BLOCKS)
+        mix_transposed(2, front, "bank5")
+        mix_transposed(2, back, "bank7")
+        finish_transposed(2, front, "bank4")
+        finish_transposed(2, back, "bank0")
         place(3)
 
-        parts = [slice(0, 320), slice(320, T)]
+        parts = [slice(0, LAST_SPLIT), slice(LAST_SPLIT, T)]
         mixed = [keep.tile([P, c.stop - c.start], F32, name="mixed%d" % c.start) for c in parts]
         y_last = [keep.tile([P, c.stop - c.start], F32, name="y_last%d" % c.start) for c in parts]
-        for h in range(2):
-            nc.vector.tensor_tensor(out=mixed[h][:], in0=z[last][:, parts[h]], in1=pages[last][:, parts[h]], op=ALU.add)
-        for h in range(2):
-            nc.vector.scalar_tensor_tensor(out=y_last[h][:], in0=mixed[h][:], scalar=0.0, in1=s_bank[:, parts[h]], op0=ALU.max, op1=ALU.add)
-            nc.sync.dma_start(out=out[P * last :, parts[h]], in_=y_last[h][:])
+        for i, cols in enumerate(parts):
+            nc.vector.tensor_tensor(out=mixed[i][:], in0=z[LAST][:, cols], in1=pages[LAST][:, cols], op=ALU.add)
+        for i, cols in enumerate(parts):
+            nc.vector.scalar_tensor_tensor(out=y_last[i][:], in0=mixed[i][:], scalar=0.0, in1=s_bank[:, cols], op0=ALU.max, op1=ALU.add)
+            nc.sync.dma_start(out=out[P * LAST :, cols], in_=y_last[i][:])

from contextlib import ExitStack

import concourse.mybir as mybir
from concourse.masks import make_identity

K, L, T, J, N = 512, 512, 512, 256, 512
FLOPS = 2 * K * N * T + 2 * L * N * T

F32 = mybir.dt.float32
BF16 = mybir.dt.bfloat16
I32 = mybir.dt.int32
U32 = mybir.dt.uint32
U16 = mybir.dt.uint16
U8 = mybir.dt.uint8
FP8X4 = mybir.dt.float8_e4m3fn_x4
FP4X4 = mybir.dt.float4_e2m1fn_x4
ALU = mybir.AluOpType
ACT = mybir.ActivationFunctionType

P = 128
PACK = 4
QUADRANTS = 4
GROUP = 16
TILES = N // P
BLOCKS = T // P
LAST = TILES - 1
SHARES = J // P
RUN = 4
ROUND_PIECES = 4
LAST_SPLIT = 320

ROW_BYTES = 4 * T
XS_BF_AT = 0
XS_RAW_AT = (2 * ROW_BYTES, 4 * ROW_BYTES)
GAP1_AT = XS_BF_AT
RELU0_AT = XS_BF_AT + ROW_BYTES
Z_LATE_AT = XS_RAW_AT[1]


def tile_list_columns_toward_partners_kernel(tc, xt_words, xt_scales, w_words, w_scales, xs, ws_words, ws_scales, sh, offs, offs2, out):
    nc = tc.nc
    with ExitStack() as ctx:
        keep = ctx.enter_context(tc.tile_pool(name="keep", bufs=1))
        reused = ctx.enter_context(tc.tile_pool(name="reused", bufs=1))
        psum = ctx.enter_context(tc.psum_pool(name="psum", bufs=1))

        own = keep.tile([P, J // GROUP], U16, name="own")
        partner = keep.tile([P, J // GROUP], U16, name="partner")
        xt_codes = keep.tile([P, T], U32, name="xt_codes", align_bytes=64)
        w_codes = keep.tile([P, 2 * N], U8, name="w_codes", align_bytes=64)
        ws_codes = keep.tile([P, N], U32, name="ws_codes", align_bytes=64)
        xt_plane = keep.tile([P, T], U8, name="xt_plane", align_bytes=64)
        w_plane = keep.tile([P, N], U8, name="w_plane", align_bytes=64)
        ws_plane = keep.tile([P, N], U8, name="ws_plane", align_bytes=64)
        xs_codes = keep.tile([P, T], U32, name="xs_codes", align_bytes=64)
        xs_plane = keep.tile([P, T], U8, name="xs_plane", align_bytes=64)
        share = keep.tile([P, J], F32, name="share")
        share_cols = keep.tile([P, SHARES], F32, name="share_cols")
        ident = keep.tile([P, P], F32, name="ident")
        pages = [keep.tile([P, T], F32, name="page%d" % m) for m in range(TILES)]
        z = [keep.tile([P, T], F32, name="z%d" % m) for m in range(2)]
        z = z + [reused.tile([P, T], F32, name="z%d" % m, offset=Z_LATE_AT + ROW_BYTES * (m - 2)) for m in range(2, TILES)]
        xs_raw = [reused.tile([P, PACK, T // 2], F32, name="xs_raw%d" % h, offset=XS_RAW_AT[h]) for h in range(2)]
        xs_bf = reused.tile([P, T, PACK], BF16, name="xs_bf", align_bytes=64, offset=XS_BF_AT)

        def load_plane_quadrant(queue, plane, scales, q):
            queue.dma_start(out=plane[32 * q : 32 * q + 4, :].bitcast(I32), in_=scales[0, 4 * q : 4 * q + 4, :].bitcast(I32))

        load_plane_quadrant(nc.sync, xt_plane, xt_scales, 0)
        load_plane_quadrant(nc.scalar, w_plane, w_scales, 0)
        nc.sync.dma_start(own[:], offs)
        load_plane_quadrant(nc.scalar, w_plane, w_scales, 1)
        nc.sync.dma_start(out=xt_codes[:].bitcast(I32), in_=xt_words[0].rearrange("p n t -> p (n t)").bitcast(I32))
        nc.scalar.dma_start(out=w_codes[:].bitcast(I32), in_=w_words[0].bitcast(I32))
        load_plane_quadrant(nc.sync, xt_plane, xt_scales, 1)
        load_plane_quadrant(nc.scalar, w_plane, w_scales, 2)
        nc.scalar.dma_start(out=share_cols[:], in_=sh[0].rearrange("(p c) -> p c", c=SHARES))
        load_plane_quadrant(nc.sync, xt_plane, xt_scales, 2)
        load_plane_quadrant(nc.sync, xt_plane, xt_scales, 3)
        load_plane_quadrant(nc.sync, w_plane, w_scales, 3)
        nc.sync.dma_start(partner[:], offs2)
        xs_view = xs.rearrange("(p j) t -> p j t", j=PACK)
        for h in range(2):
            nc.sync.dma_start(out=xs_raw[h][:], in_=xs_view[:, :, h * (T // 2) : (h + 1) * (T // 2)])
        nc.sync.dma_start(out=ws_codes[:].bitcast(I32), in_=ws_words[0].rearrange("p n t -> p (n t)").bitcast(I32))
        for q in range(QUADRANTS):
            load_plane_quadrant(nc.sync, ws_plane, ws_scales, q)

        for m in range(TILES):
            nc.vector.memset(pages[m][:], 0.0)
        make_identity(nc, ident[:])

        def first_product(m, cols, tag):
            bank = psum.tile([P, cols.stop - cols.start], F32, name="z_bank%d_%d" % (m, cols.start), tag=tag)
            nc.tensor.matmul_mx(
                out=bank[:],
                lhsT=w_codes[:, 2 * P * m : 2 * P * (m + 1)].bitcast(FP4X4),
                lhsT_scale=w_plane[:, P * m : P * (m + 1)],
                rhs=xt_codes[:, cols].bitcast(FP8X4),
                rhs_scale=xt_plane[:, cols],
                start=True,
                stop=True,
            )
            return bank

        half, quarters = slice(0, T // 2), (slice(T // 2, 3 * T // 4), slice(3 * T // 4, T))
        nc.scalar.activation(out=z[0][:, half], in_=first_product(0, half, "bank0")[:], func=ACT.Copy)
        for cols, tag in zip(quarters, ("bank4", "bank5")):
            nc.vector.tensor_copy(out=z[0][:, cols], in_=first_product(0, cols, tag)[:])
        z_banks = {m: first_product(m, slice(0, T), "bank%d" % m) for m in range(1, TILES)}

        def copy_z(m):
            nc.scalar.copy(out=z[m][:], in_=z_banks[m][:])

        copy_z(1)

        share_bank = psum.tile([P, SHARES, P], F32, name="share_bank", tag="bank0")
        for c in range(SHARES):
            nc.tensor.transpose(share_bank[:, c, :], share_cols[:, c : c + 1].to_broadcast([P, P]), ident[:])
        nc.scalar.copy(out=share[:].rearrange("p (n c) -> p n c", c=SHARES), in_=share_bank[:].rearrange("p c n -> p n c"))

        def add_transposed(bank, source, blocks, start, stop):
            for i, b in enumerate(blocks):
                nc.tensor.matmul(
                    out=bank[:, P * i : P * (i + 1)], lhsT=source[:, P * b : P * (b + 1)], rhs=ident[:],
                    is_transpose=True, start=start and i == 0, stop=stop and i == len(blocks) - 1,
                )

        picked, gaps, s_t, relu_t = {}, {}, {}, {}

        def pick_own(m):
            picked[m] = keep.tile([P, J], F32, name="picked%d" % m)
            nc.vector.tensor_copy(out=picked[m][:], in_=z[m][:].indirect(own[:]))

        def pick_partner(m):
            if m == 1:
                gaps[m] = reused.tile([P, J], F32, name="gap%d" % m, offset=GAP1_AT)
            else:
                gaps[m] = keep.tile([P, J], F32, name="gap%d" % m)
            nc.vector.tensor_tensor(out=gaps[m][:], in0=z[m][:].indirect(partner[:]), in1=picked[m][:], op=ALU.subtract)

        def place(m):
            nc.vector.tensor_tensor(out=pages[m][:].indirect(own[:]), in0=gaps[m][:], in1=share[:], op=ALU.mult)

        def quantize_xs():
            width = T // ROUND_PIECES
            per_half = ROUND_PIECES // 2
            for c in range(ROUND_PIECES):
                dst = xs_bf[:, c * width : (c + 1) * width, :]
                src = xs_raw[c // per_half][:, :, (c % per_half) * width : (c % per_half + 1) * width]
                nc.scalar.copy(out=dst.rearrange("p (c i) j -> p c j i", i=RUN), in_=src.rearrange("p j (c i) -> p c j i", i=RUN))
            nc.vector.quantize_mx(out=xs_codes[:].bitcast(FP8X4), scales=xs_plane[:], in_=xs_bf[:].rearrange("p t j -> p (t j)"))

        def second_product_transposed(m):
            bank = psum.tile([P, T], F32, name="st_bank%d" % m, tag="bank%d" % m)
            for b in range(BLOCKS):
                nc.tensor.matmul_mx(
                    out=bank[:, P * b : P * (b + 1)],
                    lhsT=xs_codes[:, P * b : P * (b + 1)].bitcast(FP8X4),
                    lhsT_scale=xs_plane[:, P * b : P * (b + 1)],
                    rhs=ws_codes[:, P * m : P * (m + 1)].bitcast(FP8X4),
                    rhs_scale=ws_plane[:, P * m : P * (m + 1)],
                    start=True,
                    stop=True,
                )
            s_t[m] = keep.tile([P, T], F32, name="s_t%d" % m)
            nc.scalar.copy(out=s_t[m][:], in_=bank[:])

        def mix_transposed(m, blocks, tag):
            width = P * len(blocks)
            bank = psum.tile([P, width], F32, name="u_bank%d_%d" % (m, blocks[0]), tag=tag)
            add_transposed(bank, z[m], blocks, True, False)
            add_transposed(bank, pages[m], blocks, False, True)
            if m == 0:
                relu = reused.tile([P, width], F32, name="relu_t0", offset=RELU0_AT)
            else:
                relu = keep.tile([P, width], F32, name="relu_t%d_%d" % (m, blocks[0]))
            nc.scalar.activation(out=relu[:], in_=bank[:], func=ACT.Relu)
            relu_t[m, blocks[0]] = relu

        def finish_transposed(m, blocks, tag):
            width = P * len(blocks)
            bank = psum.tile([P, width], F32, name="y_bank%d_%d" % (m, blocks[0]), tag=tag)
            add_transposed(bank, s_t[m], blocks, True, False)
            add_transposed(bank, relu_t[m, blocks[0]], range(len(blocks)), False, True)
            y = keep.tile([P, width], F32, name="y%d_%d" % (m, blocks[0]))
            nc.scalar.copy(out=y[:], in_=bank[:])
            nc.scalar.dma_start(out=out[P * m : P * (m + 1), P * blocks[0] : P * blocks[0] + width], in_=y[:])

        whole = range(BLOCKS)
        pick_own(0)
        pick_partner(0)
        pick_own(1)
        place(0)
        quantize_xs()
        pick_partner(1)
        copy_z(2)
        copy_z(3)
        mix_transposed(0, whole, "bank4")
        pick_own(2)
        place(1)
        pick_partner(2)
        for m in range(LAST):
            second_product_transposed(m)
        finish_transposed(0, whole, "bank6")
        mix_transposed(1, whole, "bank5")
        finish_transposed(1, whole, "bank7")
        s_bank = psum.tile([P, T], F32, name="s_bank", tag="bank%d" % LAST)
        nc.tensor.matmul_mx(
            out=s_bank[:],
            lhsT=ws_codes[:, P * LAST :].bitcast(FP8X4),
            lhsT_scale=ws_plane[:, P * LAST :],
            rhs=xs_codes[:].bitcast(FP8X4),
            rhs_scale=xs_plane[:],
            start=True,
            stop=True,
        )
        pick_own(3)
        place(2)
        pick_partner(3)
        front, back = range(0, BLOCKS // 2), range(BLOCKS // 2, BLOCKS)
        mix_transposed(2, front, "bank5")
        mix_transposed(2, back, "bank7")
        finish_transposed(2, front, "bank4")
        finish_transposed(2, back, "bank0")
        place(3)

        parts = [slice(0, LAST_SPLIT), slice(LAST_SPLIT, T)]
        mixed = [keep.tile([P, c.stop - c.start], F32, name="mixed%d" % c.start) for c in parts]
        y_last = [keep.tile([P, c.stop - c.start], F32, name="y_last%d" % c.start) for c in parts]
        for i, cols in enumerate(parts):
            nc.vector.tensor_tensor(out=mixed[i][:], in0=z[LAST][:, cols], in1=pages[LAST][:, cols], op=ALU.add)
        for i, cols in enumerate(parts):
            nc.vector.scalar_tensor_tensor(out=y_last[i][:], in0=mixed[i][:], scalar=0.0, in1=s_bank[:, cols], op0=ALU.max, op1=ALU.add)
            nc.sync.dma_start(out=out[P * LAST :, cols], in_=y_last[i][:])
